import numpy as np
import ml_dtypes


def mxq(x, axis, fmt="e4m3"):
    dtype, down = {"e4m3": (ml_dtypes.float8_e4m3fn, 7), "e5m2": (ml_dtypes.float8_e5m2, 14)}[fmt]
    v = np.moveaxis(np.asarray(x, np.float32).astype(ml_dtypes.bfloat16).astype(np.float64), axis, -1)
    blocks = v.reshape(v.shape[:-1] + (-1, 32))
    amax = np.abs(blocks).max(-1, keepdims=True)
    byte = np.maximum(np.where(amax > 0, np.frexp(amax)[1] - 1 + 127, 0) - down, 1)
    scale = np.exp2(byte - 127.0)
    codes = (blocks / scale).astype(np.float32).astype(dtype).astype(np.float64)
    return np.moveaxis((codes * scale).reshape(v.shape), -1, axis)


WIDE = False


def mx_kscale(k):
    if not WIDE:
        return np.ones(k)
    levels = np.array([10, -10, 5, -5, 0])
    if k % 512:
        return np.exp2(np.random.permutation(np.resize(levels, k // 32))).repeat(32)
    a = np.empty((k // 512, 16))
    for p in range(k // 512):
        a[p, :8] = np.random.permutation(np.resize(levels, 8))
        for g in range(8):
            far = levels[np.abs(levels - a[p, g]) >= 10]
            a[p, g + 8] = far[np.random.randint(len(far))]
    return np.exp2(a.ravel()).repeat(32)


def f64(x):
    return np.asarray(x).astype(np.float64)


def striped(idx):
    return np.tile(idx.reshape(-1, 16).T, (8, 1)).astype(np.uint16)


def unstriped(offs):
    return offs[:16].T.reshape(-1).astype(np.int64)


def striped8(idx):
    return np.concatenate([x.reshape(-1, 16).T for x in idx]).astype(np.uint16)


def runs(offs, k):
    lists = np.stack([offs[16 * r : 16 * r + 16].T.reshape(-1) for r in range(8)]).astype(np.int64)
    return lists[np.arange(k) % 512 // 64]


def pack_weight(w):
    k, n = w.shape
    w = f64(np.asarray(w, np.float32).astype(ml_dtypes.bfloat16)).reshape(k // 32, 32, n)
    amax = np.abs(w).max(1)
    byte = np.clip(np.where(amax > 0, np.frexp(amax)[1] - 1 + 127 - 7, 1), 1, 254)
    scaled = (w * np.exp2(127.0 - byte)[:, None, :]).reshape(k, n).astype(np.float32)
    words = np.ascontiguousarray(scaled.reshape(k // 512, 128, 4, n).transpose(0, 1, 3, 2)).astype(ml_dtypes.float8_e4m3fn).view(np.uint8)
    return words, np.ascontiguousarray(byte.astype(np.uint8).reshape(k // 512, 16, n))


def unpack_weight(words, scales):
    g, p, n, _ = words.shape
    vals = np.ascontiguousarray(words).view(ml_dtypes.float8_e4m3fn).astype(np.float64) * np.repeat(np.exp2(scales.astype(np.float64) - 127.0), 8, axis=1)[..., None]
    return vals.transpose(0, 1, 3, 2).reshape(g * 512, n)


K, T, S, H, C = 512, 2048, 512, 512, 512


def setup_inputs():
    n = np.random.standard_normal
    s = mx_kscale(K)[:, None]
    packed_xT = pack_weight(n((K, T)) * s)
    return {
        "x_words": packed_xT[0],
        "x_scales": packed_xT[1],
        "w1": (n((K, H)) / np.sqrt(K) / s).astype(np.float32),
        "gs": (np.random.uniform(0.5, 1.5, (K, 1)) / s).astype(np.float32),
        "offs": striped(np.random.permutation(T)[:S]),
        "n1": striped8(np.stack([np.random.permutation(S) for _ in range(8)])),
        "n2": striped8(np.stack([np.random.permutation(S) for _ in range(8)])),
        "ca": striped(np.random.permutation(T)[:C]),
        "cb": striped(np.random.permutation(T)[:C]),
        "n3": striped8(np.stack([np.random.permutation(S) for _ in range(8)])),
        "n4": striped8(np.stack([np.random.permutation(S) for _ in range(8)])),
    }


def reference(x_words, x_scales, w1, gs, offs, n1, n2, ca, cb, n3, n4):
    x_ca = unpack_weight(x_words, x_scales)[:, unstriped(ca)]
    xq = unpack_weight(x_words, x_scales)[:, unstriped(offs)]
    y = mxq(f64(w1), 0, "e4m3").T @ xq
    st = np.maximum(y, y[np.arange(H)[:, None], runs(n1, H)])
    z = f64(gs) * (st[np.arange(H)[:, None], runs(n2, H)] - (0.5 * y))
    zq = mxq(z, 0, "e4m3")
    a = 0.0625 * (x_ca.T @ zq)
    x_cb = unpack_weight(x_words, x_scales)[:, unstriped(cb)]
    b = 0.0625 * (x_cb.T @ zq)
    return a[np.arange(C)[:, None], runs(n3, C)] - (np.tanh(b) * (b[np.arange(C)[:, None], runs(n4, C)]))

@@ -1,0 +1,203 @@
+from contextlib import ExitStack
+
+import concourse.mybir as mybir
+
+K, T, S, H, C = 512, 2048, 512, 512, 512
+FLOPS = 2 * K * S * (H + 2 * C)
+
+F32 = mybir.dt.float32
+BF16 = mybir.dt.bfloat16
+I32 = mybir.dt.int32
+U32 = mybir.dt.uint32
+U16 = mybir.dt.uint16
+U8 = mybir.dt.uint8
+FP8X4 = mybir.dt.float8_e4m3fn_x4
+ACT = mybir.ActivationFunctionType
+ALU = mybir.AluOpType
+
+P = 128
+PACK = 4
+HALF = S // 2
+WIDE = 2 * S
+
+
+def tile_picked_ccmpsoftbhopb_none_p_kernel(tc, x_words, x_scales, w1, gs, offs, n1, n2, ca, cb, n3, n4, out):
+    nc = tc.nc
+    with ExitStack() as ctx:
+        lists = ctx.enter_context(tc.tile_pool(name="lists", bufs=1))
+        keep = ctx.enter_context(tc.tile_pool(name="keep", bufs=1))
+        psum = ctx.enter_context(tc.psum_pool(name="psum", bufs=1))
+
+        def load_list(src, name):
+            tile = lists.tile([P, S // 16], U16, name=name)
+            nc.sync.dma_start(tile[:], src)
+            return tile
+
+        table_scales = keep.tile([P, T], U8, name="table_scales", align_bytes=64)
+        nc.vector.memset(table_scales[:].bitcast(I32), 0)
+        warm = keep.tile([P, 2], F32, name="warm")
+        nc.vector.memset(warm[:, 0:1], 0.0)
+
+        offs_sb = load_list(offs, "offs_sb")
+        cb_sb = load_list(cb, "cb_sb")
+        ca_sb = load_list(ca, "ca_sb")
+        for q in range(4):
+            nc.sync.dma_start(table_scales[32 * q : 32 * q + 4, :].bitcast(I32), x_scales[0, 4 * q : 4 * q + 4, :].bitcast(I32))
+        nc.scalar.activation(warm[:, 1:2], warm[:, 0:1], ACT.Tanh)
+        w_rows = w1.rearrange("(p j) c -> p j c", j=PACK)
+        w_raw = []
+        for h in range(2):
+            tile = keep.tile([P, PACK, H // 2], F32, name=f"w_raw{h}")
+            nc.sync.dma_start(tile[:], w_rows[:, :, h * H // 2 : (h + 1) * H // 2])
+            w_raw.append(tile)
+        table_words = keep.tile([P, T], I32, name="table_words", align_bytes=64)
+        nc.sync.dma_start(table_words[:], x_words[0].rearrange("p n t -> p (n t)").bitcast(I32))
+        n1_sb = load_list(n1, "n1_sb")
+        gs_sb = keep.tile([P, PACK], F32, name="gs_sb")
+        nc.sync.dma_start(gs_sb[:], gs.rearrange("(p t) o -> p (t o)", t=PACK))
+        n2_sb = load_list(n2, "n2_sb")
+        n4_sb = load_list(n4, "n4_sb")
+        n3_sb = load_list(n3, "n3_sb")
+
+        def gather_scales(lst, name, tag):
+            tile = keep.tile([P, S], U8, name=name, tag=tag, align_bytes=64)
+            nc.vector.tensor_copy(tile[:], table_scales[:].indirect(lst[:]))
+            return tile
+
+        def gather_words(lst, name, tag):
+            tile = keep.tile([P, S], U32, name=name, tag=tag, align_bytes=64)
+            nc.vector.tensor_copy(tile[:], table_words[:].bitcast(U32).indirect(lst[:]))
+            return tile
+
+        def gather_words_dealt(lst, name, tag):
+            tile = keep.tile([P, S], U32, name=name, tag=tag, align_bytes=64)
+            nc.vector.tensor_copy(tile[:].rearrange("p (t g q) -> p g t q", t=PACK, q=PACK), table_words[:].bitcast(U32).indirect(lst[:]))
+            return tile
+
+        def deal(src, name):
+            tile = keep.tile([P, S], U8, name=name, align_bytes=64)
+            nc.vector.tensor_copy(tile[:].bitcast(I32).rearrange("p (t g) -> p t g", t=PACK), src[:].bitcast(I32).rearrange("p (g t) -> p t g", t=PACK))
+            return tile
+
+        xq_scales = gather_scales(offs_sb, "xq_scales", "xq_scales")
+        cb_scales_raw = gather_scales(cb_sb, "cb_scales_raw", "cb_scales_raw")
+        cb_scales = deal(cb_scales_raw, "cb_scales")
+
+        w_bf = keep.tile([P, PACK, P, PACK], BF16, name="w_bf", tag="w_bf", align_bytes=64)
+        for h in range(2):
+            nc.scalar.copy(w_bf[:, :, h * P // 2 : (h + 1) * P // 2, :].rearrange("p t m j -> p m t j"), w_raw[h][:].rearrange("p j (m t) -> p m t j", t=PACK))
+        half_gs = keep.tile([P, PACK], F32, name="half_gs")
+        nc.scalar.activation(half_gs[:], gs_sb[:], ACT.Copy, scale=0.5)
+
+        w_codes = keep.tile([P, H], U32, name="w_codes", align_bytes=64)
+        w_scales = keep.tile([P, H], U8, name="w_scales", align_bytes=64)
+        nc.vector.quantize_mx(out=w_codes[:].bitcast(FP8X4), scales=w_scales[:], in_=w_bf[:].rearrange("p t m j -> p (t m j)"))
+        xq_words = gather_words(offs_sb, "xq_words", "xq_words")
+        cb_words = gather_words_dealt(cb_sb, "cb_words", "w_bf")
+
+        y_ps = []
+        for t in range(PACK):
+            bank = psum.tile([P, S], F32, name=f"y_ps{t}", tag=f"bank{t}")
+            cols = slice(t * P, (t + 1) * P)
+            nc.tensor.matmul_mx(out=bank[:], lhsT=w_codes[:, cols].bitcast(FP8X4), lhsT_scale=w_scales[:, cols],
+                                rhs=xq_words[:].bitcast(FP8X4), rhs_scale=xq_scales[:], start=True, stop=True)
+            y_ps.append(bank)
+
+        y_win, half_y, st_win = [], [], []
+        for t in range(PACK):
+            win = keep.tile([P, WIDE], F32, name=f"y_win{t}")
+            nc.scalar.copy(win[:, :S], y_ps[t][:])
+            y_win.append(win)
+        for t in range(PACK):
+            tile = keep.tile([P, S], F32, name=f"half_y{t}", tag=f"half_y{t}", align_bytes=64)
+            nc.scalar.activation(tile[:], y_ps[t][:], ACT.Copy, scale=half_gs[:, t : t + 1])
+            half_y.append(tile)
+
+        hop = []
+
+        def fetch_y(t):
+            tile = keep.tile([P, S], F32, name=f"hop{t}")
+            nc.vector.tensor_copy(tile[:], y_win[t][:].indirect(n1_sb[:]))
+            hop.append(tile)
+
+        def larger(t):
+            st = keep.tile([P, S], F32, name=f"st{t}")
+            nc.vector.tensor_tensor(st[:], hop[t][:], y_win[t][:, :S], ALU.max)
+            win = keep.tile([P, S], F32, name=f"st_win{t}")
+            nc.scalar.activation(win[:], st[:], ACT.Copy, scale=gs_sb[:, t : t + 1])
+            st_win.append(win)
+
+        fetch_y(0)
+        for t in range(1, PACK):
+            fetch_y(t)
+            larger(t - 1)
+        larger(PACK - 1)
+
+        z_bf = []
+        for h in range(2):
+            cols = slice(h * HALF, (h + 1) * HALF)
+            z32 = keep.tile([P, PACK, HALF], F32, name=f"z32_{h}")
+            for t in range(PACK):
+                nc.vector.tensor_tensor(z32[:, t, :], st_win[t][:].indirect(n2_sb[:, h * HALF // 16 : (h + 1) * HALF // 16]), half_y[t][:, cols], ALU.subtract)
+            zb = keep.tile([P, HALF, PACK], BF16, name=f"z_bf{h}", tag=f"z_bf{h}", align_bytes=64)
+            nc.scalar.copy(zb[:].rearrange("p (c i) t -> p c t i", i=4), z32[:].rearrange("p t (c i) -> p c t i", i=4))
+            z_bf.append(zb)
+
+        z_codes, z_scales = [], []
+
+        def quantise_z(h):
+            codes = keep.tile([P, HALF], U32, name=f"z_codes{h}", align_bytes=64)
+            scales = keep.tile([P, HALF], U8, name=f"z_scales{h}", align_bytes=64)
+            nc.vector.quantize_mx(out=codes[:].bitcast(FP8X4), scales=scales[:], in_=z_bf[h][:].rearrange("p c t -> p (c t)"))
+            z_codes.append(codes)
+            z_scales.append(scales)
+
+        quantise_z(0)
+        ca_words = gather_words_dealt(ca_sb, "ca_words", "half_y3")
+        quantise_z(1)
+        ca_scales_raw = gather_scales(ca_sb, "ca_scales_raw", "z_bf1")
+        ca_scales = deal(ca_scales_raw, "ca_scales")
+
+        def score(words, scales, dest, t, h):
+            rows = slice(t * P, (t + 1) * P)
+            nc.tensor.matmul_mx(out=dest, lhsT=words[:, rows].bitcast(FP8X4), lhsT_scale=scales[:, rows],
+                                rhs=z_codes[h][:].bitcast(FP8X4), rhs_scale=z_scales[h][:], start=True, stop=True)
+
+        halves = [slice(h * HALF, (h + 1) * HALF) for h in range(2)]
+        b_early = psum.tile([P, S], F32, name="b_early", tag="bank0")
+        b_ps = [psum.tile([P, S], F32, name=f"b_ps{t}", tag=f"bank{PACK + t}") for t in range(PACK)]
+        for h in range(2):
+            for t in range(PACK):
+                bank = b_early if (t, h) == (0, 0) else b_ps[t]
+                score(cb_words, cb_scales, bank[:, halves[h]], t, h)
+
+        out_rows = out.rearrange("(g t q) j -> t g q j", t=PACK, q=PACK)
+        prod = []
+
+        def b_side(t):
+            b_win = keep.tile([P, WIDE], F32, name=f"b_win{t}")
+            gate = keep.tile([P, S], F32, name=f"gate{t}")
+            pieces = [(b_early, halves[0]), (b_ps[0], halves[1])] if t == 0 else [(b_ps[t], slice(0, S))]
+            for bank, cols in pieces:
+                nc.scalar.activation(b_win[:, cols], bank[:, cols], ACT.Copy, scale=0.0625)
+                nc.scalar.activation(gate[:, cols], bank[:, cols], ACT.Tanh, scale=0.0625)
+            tile = keep.tile([P, S], F32, name=f"prod{t}")
+            nc.vector.tensor_tensor(tile[:], b_win[:].indirect(n4_sb[:]), gate[:], ALU.mult)
+            prod.append(tile)
+
+        def a_side(t):
+            bank = psum.tile([P, S], F32, name=f"a_ps{t}", tag=f"bank{(t + 1) % PACK}")
+            for h in range(2):
+                score(ca_words, ca_scales, bank[:, halves[h]], t, h)
+            win = keep.tile([P, WIDE], F32, name=f"a_win{t}")
+            nc.scalar.activation(win[:, :S], bank[:], ACT.Copy, scale=0.0625)
+            for n, cols in enumerate(halves if t == PACK - 1 else [slice(0, S)]):
+                res = keep.tile([P, cols.stop - cols.start], F32, name=f"res{t}_{n}")
+                nc.vector.tensor_tensor(res[:], win[:].indirect(n3_sb[:, cols.start // 16 : cols.stop // 16]), prod[t][:, cols], ALU.subtract)
+                nc.sync.dma_start(out_rows[t][:, :, cols], res[:])
+
+        b_side(0)
+        for t in range(1, PACK):
+            b_side(t)
+            a_side(t - 1)
+        a_side(PACK - 1)

@@ -19,6 +19,7 @@ P = 128
 PACK = 4
 HALF = S // 2
 WIDE = 2 * S
+PIECES = [slice(0, 320), slice(320, 512)]
 
 
 def tile_picked_ccmpsoftbhopb_none_p_kernel(tc, x_words, x_scales, w1, gs, offs, n1, n2, ca, cb, n3, n4, out):
@@ -59,9 +60,9 @@ def tile_picked_ccmpsoftbhopb_none_p_kernel(tc, x_words, x_scales, w1, gs, offs,
         n4_sb = load_list(n4, "n4_sb")
         n3_sb = load_list(n3, "n3_sb")
 
-        def gather_scales(lst, name, tag):
-            tile = keep.tile([P, S], U8, name=name, tag=tag, align_bytes=64)
-            nc.vector.tensor_copy(tile[:], table_scales[:].indirect(lst[:]))
+        def gather_scales(lst, name, tag, entries=slice(0, S)):
+            tile = keep.tile([P, entries.stop - entries.start], U8, name=name, tag=tag, align_bytes=64)
+            nc.vector.tensor_copy(tile[:], table_scales[:].indirect(lst[:, entries.start // 16 : entries.stop // 16]))
             return tile
 
         def gather_words(lst, name, tag):
@@ -74,14 +75,18 @@ def tile_picked_ccmpsoftbhopb_none_p_kernel(tc, x_words, x_scales, w1, gs, offs,
             nc.vector.tensor_copy(tile[:].rearrange("p (t g q) -> p g t q", t=PACK, q=PACK), table_words[:].bitcast(U32).indirect(lst[:]))
             return tile
 
-        def deal(src, name):
-            tile = keep.tile([P, S], U8, name=name, align_bytes=64)
-            nc.vector.tensor_copy(tile[:].bitcast(I32).rearrange("p (t g) -> p t g", t=PACK), src[:].bitcast(I32).rearrange("p (g t) -> p t g", t=PACK))
-            return tile
+        def deal(src, dst, entries=slice(0, S)):
+            groups = slice(entries.start // 16, entries.stop // 16)
+            nc.vector.tensor_copy(dst[:].bitcast(I32).rearrange("p (t g) -> p t g", t=PACK)[:, :, groups], src[:].bitcast(I32).rearrange("p (g t) -> p t g", t=PACK))
 
         xq_scales = gather_scales(offs_sb, "xq_scales", "xq_scales")
         cb_scales_raw = gather_scales(cb_sb, "cb_scales_raw", "cb_scales_raw")
-        cb_scales = deal(cb_scales_raw, "cb_scales")
+        halves = [slice(h * HALF, (h + 1) * HALF) for h in range(2)]
+        ca_scales_raw0 = gather_scales(ca_sb, "ca_scales_raw0", "ca_scales_raw0", halves[0])
+        cb_scales = keep.tile([P, S], U8, name="cb_scales", align_bytes=64)
+        ca_scales = keep.tile([P, S], U8, name="ca_scales", align_bytes=64)
+        deal(cb_scales_raw, cb_scales)
+        deal(ca_scales_raw0, ca_scales, halves[0])
 
         w_bf = keep.tile([P, PACK, P, PACK], BF16, name="w_bf", tag="w_bf", align_bytes=64)
         for h in range(2):
@@ -95,22 +100,19 @@ def tile_picked_ccmpsoftbhopb_none_p_kernel(tc, x_words, x_scales, w1, gs, offs,
         xq_words = gather_words(offs_sb, "xq_words", "xq_words")
         cb_words = gather_words_dealt(cb_sb, "cb_words", "w_bf")
 
-        y_ps = []
-        for t in range(PACK):
-            bank = psum.tile([P, S], F32, name=f"y_ps{t}", tag=f"bank{t}")
-            cols = slice(t * P, (t + 1) * P)
-            nc.tensor.matmul_mx(out=bank[:], lhsT=w_codes[:, cols].bitcast(FP8X4), lhsT_scale=w_scales[:, cols],
-                                rhs=xq_words[:].bitcast(FP8X4), rhs_scale=xq_scales[:], start=True, stop=True)
-            y_ps.append(bank)
-
         y_win, half_y, st_win = [], [], []
         for t in range(PACK):
             win = keep.tile([P, WIDE], F32, name=f"y_win{t}")
-            nc.scalar.copy(win[:, :S], y_ps[t][:])
+            rows = slice(t * P, (t + 1) * P)
+            for n, cols in enumerate(halves if t == 0 else [slice(0, S)]):
+                bank = psum.tile([P, S], F32, name=f"y_ps{t}_{n}", tag=f"bank{t + PACK * n}")
+                nc.tensor.matmul_mx(out=bank[:, cols], lhsT=w_codes[:, rows].bitcast(FP8X4), lhsT_scale=w_scales[:, rows],
+                                    rhs=xq_words[:, cols].bitcast(FP8X4), rhs_scale=xq_scales[:, cols], start=True, stop=True)
+                nc.scalar.copy(win[:, cols], bank[:, cols])
             y_win.append(win)
         for t in range(PACK):
             tile = keep.tile([P, S], F32, name=f"half_y{t}", tag=f"half_y{t}", align_bytes=64)
-            nc.scalar.activation(tile[:], y_ps[t][:], ACT.Copy, scale=half_gs[:, t : t + 1])
+            nc.scalar.activation(tile[:], y_win[t][:, :S], ACT.Copy, scale=half_gs[:, t : t + 1])
             half_y.append(tile)
 
         hop = []
@@ -121,10 +123,10 @@ def tile_picked_ccmpsoftbhopb_none_p_kernel(tc, x_words, x_scales, w1, gs, offs,
             hop.append(tile)
 
         def larger(t):
-            st = keep.tile([P, S], F32, name=f"st{t}")
+            st = keep.tile([P, S], F32, name=f"st{t}", tag=f"st{t}")
             nc.vector.tensor_tensor(st[:], hop[t][:], y_win[t][:, :S], ALU.max)
-            win = keep.tile([P, S], F32, name=f"st_win{t}")
-            nc.scalar.activation(win[:], st[:], ACT.Copy, scale=gs_sb[:, t : t + 1])
+            win = keep.tile([P, 768], F32, name=f"st_win{t}")
+            nc.scalar.activation(win[:, :S], st[:], ACT.Copy, scale=gs_sb[:, t : t + 1])
             st_win.append(win)
 
         fetch_y(0)
@@ -133,62 +135,58 @@ def tile_picked_ccmpsoftbhopb_none_p_kernel(tc, x_words, x_scales, w1, gs, offs,
             larger(t - 1)
         larger(PACK - 1)
 
-        z_bf = []
-        for h in range(2):
-            cols = slice(h * HALF, (h + 1) * HALF)
-            z32 = keep.tile([P, PACK, HALF], F32, name=f"z32_{h}")
+        z_bf = [keep.tile([P, HALF * PACK], BF16, name=f"z_bf{h}", tag=f"z_bf{h}", align_bytes=64) for h in range(2)]
+        for n, piece in enumerate(PIECES):
+            z32 = keep.tile([P, PACK, piece.stop - piece.start], F32, name=f"z32_{n}", tag=("z32", f"st{PACK - 1}")[n])
             for t in range(PACK):
-                nc.vector.tensor_tensor(z32[:, t, :], st_win[t][:].indirect(n2_sb[:, h * HALF // 16 : (h + 1) * HALF // 16]), half_y[t][:, cols], ALU.subtract)
-            zb = keep.tile([P, HALF, PACK], BF16, name=f"z_bf{h}", tag=f"z_bf{h}", align_bytes=64)
-            nc.scalar.copy(zb[:].rearrange("p (c i) t -> p c t i", i=4), z32[:].rearrange("p t (c i) -> p c t i", i=4))
-            z_bf.append(zb)
+                nc.vector.tensor_tensor(z32[:, t, :], st_win[t][:].indirect(n2_sb[:, piece.start // 16 : piece.stop // 16]), half_y[t][:, piece], ALU.subtract)
+            for h, half in enumerate(halves):
+                first, last = max(piece.start, half.start), min(piece.stop, half.stop)
+                if first < last:
+                    nc.scalar.copy(z_bf[h][:, PACK * (first - half.start) : PACK * (last - half.start)].rearrange("p (c i t) -> p c t i", i=4, t=PACK),
+                                   z32[:, :, first - piece.start : last - piece.start].rearrange("p t (c i) -> p c t i", i=4))
 
-        z_codes, z_scales = [], []
+        z_codes = keep.tile([P, S], U32, name="z_codes", align_bytes=64)
+        z_scales = keep.tile([P, S], U8, name="z_scales", align_bytes=64)
 
         def quantise_z(h):
-            codes = keep.tile([P, HALF], U32, name=f"z_codes{h}", align_bytes=64)
-            scales = keep.tile([P, HALF], U8, name=f"z_scales{h}", align_bytes=64)
-            nc.vector.quantize_mx(out=codes[:].bitcast(FP8X4), scales=scales[:], in_=z_bf[h][:].rearrange("p c t -> p (c t)"))
-            z_codes.append(codes)
-            z_scales.append(scales)
+            nc.vector.quantize_mx(out=z_codes[:, halves[h]].bitcast(FP8X4), scales=z_scales[:, halves[h]], in_=z_bf[h][:])
+
+        def score(words, scales, bank, t, cols):
+            rows = slice(t * P, (t + 1) * P)
+            nc.tensor.matmul_mx(out=bank[:, cols], lhsT=words[:, rows].bitcast(FP8X4), lhsT_scale=scales[:, rows],
+                                rhs=z_codes[:, cols].bitcast(FP8X4), rhs_scale=z_scales[:, cols], start=True, stop=True)
+
+        b_win = [keep.tile([P, WIDE], F32, name=f"b_win{t}") for t in range(PACK)]
+        gate = [keep.tile([P, S], F32, name=f"gate{t}") for t in range(PACK)]
+
+        def score_b(t, cols, bank_no):
+            bank = psum.tile([P, S], F32, name=f"b_ps{t}_{cols.start}", tag=f"bank{bank_no}")
+            score(cb_words, cb_scales, bank, t, cols)
+            nc.scalar.activation(b_win[t][:, cols], bank[:, cols], ACT.Copy, scale=0.0625)
+            nc.scalar.activation(gate[t][:, cols], bank[:, cols], ACT.Tanh, scale=0.0625)
 
         quantise_z(0)
-        ca_words = gather_words_dealt(ca_sb, "ca_words", "half_y3")
+        score_b(0, halves[0], 0)
+        ca_scales_raw1 = gather_scales(ca_sb, "ca_scales_raw1", "half_y3", halves[1])
         quantise_z(1)
-        ca_scales_raw = gather_scales(ca_sb, "ca_scales_raw", "z_bf1")
-        ca_scales = deal(ca_scales_raw, "ca_scales")
-
-        def score(words, scales, dest, t, h):
-            rows = slice(t * P, (t + 1) * P)
-            nc.tensor.matmul_mx(out=dest, lhsT=words[:, rows].bitcast(FP8X4), lhsT_scale=scales[:, rows],
-                                rhs=z_codes[h][:].bitcast(FP8X4), rhs_scale=z_scales[h][:], start=True, stop=True)
-
-        halves = [slice(h * HALF, (h + 1) * HALF) for h in range(2)]
-        b_early = psum.tile([P, S], F32, name="b_early", tag="bank0")
-        b_ps = [psum.tile([P, S], F32, name=f"b_ps{t}", tag=f"bank{PACK + t}") for t in range(PACK)]
-        for h in range(2):
-            for t in range(PACK):
-                bank = b_early if (t, h) == (0, 0) else b_ps[t]
-                score(cb_words, cb_scales, bank[:, halves[h]], t, h)
+        score_b(0, halves[1], PACK)
+        deal(ca_scales_raw1, ca_scales, halves[1])
+        ca_words = gather_words_dealt(ca_sb, "ca_words", "z_bf1")
 
         out_rows = out.rearrange("(g t q) j -> t g q j", t=PACK, q=PACK)
         prod = []
 
         def b_side(t):
-            b_win = keep.tile([P, WIDE], F32, name=f"b_win{t}")
-            gate = keep.tile([P, S], F32, name=f"gate{t}")
-            pieces = [(b_early, halves[0]), (b_ps[0], halves[1])] if t == 0 else [(b_ps[t], slice(0, S))]
-            for bank, cols in pieces:
-                nc.scalar.activation(b_win[:, cols], bank[:, cols], ACT.Copy, scale=0.0625)
-                nc.scalar.activation(gate[:, cols], bank[:, cols], ACT.Tanh, scale=0.0625)
+            if t > 0:
+                score_b(t, slice(0, S), PACK + t)
             tile = keep.tile([P, S], F32, name=f"prod{t}")
-            nc.vector.tensor_tensor(tile[:], b_win[:].indirect(n4_sb[:]), gate[:], ALU.mult)
+            nc.vector.tensor_tensor(tile[:], b_win[t][:].indirect(n4_sb[:]), gate[t][:], ALU.mult)
             prod.append(tile)
 
         def a_side(t):
             bank = psum.tile([P, S], F32, name=f"a_ps{t}", tag=f"bank{(t + 1) % PACK}")
-            for h in range(2):
-                score(ca_words, ca_scales, bank[:, halves[h]], t, h)
+            score(ca_words, ca_scales, bank, t, slice(0, S))
             win = keep.tile([P, WIDE], F32, name=f"a_win{t}")
             nc.scalar.activation(win[:, :S], bank[:], ACT.Copy, scale=0.0625)
             for n, cols in enumerate(halves if t == PACK - 1 else [slice(0, S)]):

from contextlib import ExitStack

import concourse.mybir as mybir

K, T, S, H, C = 512, 2048, 512, 512, 512
FLOPS = 2 * K * S * (H + 2 * C)

F32 = mybir.dt.float32
BF16 = mybir.dt.bfloat16
I32 = mybir.dt.int32
U32 = mybir.dt.uint32
U16 = mybir.dt.uint16
U8 = mybir.dt.uint8
FP8X4 = mybir.dt.float8_e4m3fn_x4
ACT = mybir.ActivationFunctionType
ALU = mybir.AluOpType

P = 128
PACK = 4
HALF = S // 2
WIDE = 2 * S
PIECES = [slice(0, 320), slice(320, 512)]


def tile_picked_ccmpsoftbhopb_none_p_kernel(tc, x_words, x_scales, w1, gs, offs, n1, n2, ca, cb, n3, n4, out):
    nc = tc.nc
    with ExitStack() as ctx:
        lists = ctx.enter_context(tc.tile_pool(name="lists", bufs=1))
        keep = ctx.enter_context(tc.tile_pool(name="keep", bufs=1))
        psum = ctx.enter_context(tc.psum_pool(name="psum", bufs=1))

        def load_list(src, name):
            tile = lists.tile([P, S // 16], U16, name=name)
            nc.sync.dma_start(tile[:], src)
            return tile

        table_scales = keep.tile([P, T], U8, name="table_scales", align_bytes=64)
        nc.vector.memset(table_scales[:].bitcast(I32), 0)
        warm = keep.tile([P, 2], F32, name="warm")
        nc.vector.memset(warm[:, 0:1], 0.0)

        offs_sb = load_list(offs, "offs_sb")
        cb_sb = load_list(cb, "cb_sb")
        ca_sb = load_list(ca, "ca_sb")
        for q in range(4):
            nc.sync.dma_start(table_scales[32 * q : 32 * q + 4, :].bitcast(I32), x_scales[0, 4 * q : 4 * q + 4, :].bitcast(I32))
        nc.scalar.activation(warm[:, 1:2], warm[:, 0:1], ACT.Tanh)
        w_rows = w1.rearrange("(p j) c -> p j c", j=PACK)
        w_raw = []
        for h in range(2):
            tile = keep.tile([P, PACK, H // 2], F32, name=f"w_raw{h}")
            nc.sync.dma_start(tile[:], w_rows[:, :, h * H // 2 : (h + 1) * H // 2])
            w_raw.append(tile)
        table_words = keep.tile([P, T], I32, name="table_words", align_bytes=64)
        nc.sync.dma_start(table_words[:], x_words[0].rearrange("p n t -> p (n t)").bitcast(I32))
        n1_sb = load_list(n1, "n1_sb")
        gs_sb = keep.tile([P, PACK], F32, name="gs_sb")
        nc.sync.dma_start(gs_sb[:], gs.rearrange("(p t) o -> p (t o)", t=PACK))
        n2_sb = load_list(n2, "n2_sb")
        n4_sb = load_list(n4, "n4_sb")
        n3_sb = load_list(n3, "n3_sb")

        def gather_scales(lst, name, tag, entries=slice(0, S)):
            tile = keep.tile([P, entries.stop - entries.start], U8, name=name, tag=tag, align_bytes=64)
            nc.vector.tensor_copy(tile[:], table_scales[:].indirect(lst[:, entries.start // 16 : entries.stop // 16]))
            return tile

        def gather_words(lst, name, tag):
            tile = keep.tile([P, S], U32, name=name, tag=tag, align_bytes=64)
            nc.vector.tensor_copy(tile[:], table_words[:].bitcast(U32).indirect(lst[:]))
            return tile

        def gather_words_dealt(lst, name, tag):
            tile = keep.tile([P, S], U32, name=name, tag=tag, align_bytes=64)
            nc.vector.tensor_copy(tile[:].rearrange("p (t g q) -> p g t q", t=PACK, q=PACK), table_words[:].bitcast(U32).indirect(lst[:]))
            return tile

        def deal(src, dst, entries=slice(0, S)):
            groups = slice(entries.start // 16, entries.stop // 16)
            nc.vector.tensor_copy(dst[:].bitcast(I32).rearrange("p (t g) -> p t g", t=PACK)[:, :, groups], src[:].bitcast(I32).rearrange("p (g t) -> p t g", t=PACK))

        xq_scales = gather_scales(offs_sb, "xq_scales", "xq_scales")
        cb_scales_raw = gather_scales(cb_sb, "cb_scales_raw", "cb_scales_raw")
        halves = [slice(h * HALF, (h + 1) * HALF) for h in range(2)]
        ca_scales_raw0 = gather_scales(ca_sb, "ca_scales_raw0", "ca_scales_raw0", halves[0])
        cb_scales = keep.tile([P, S], U8, name="cb_scales", align_bytes=64)
        ca_scales = keep.tile([P, S], U8, name="ca_scales", align_bytes=64)
        deal(cb_scales_raw, cb_scales)
        deal(ca_scales_raw0, ca_scales, halves[0])

        w_bf = keep.tile([P, PACK, P, PACK], BF16, name="w_bf", tag="w_bf", align_bytes=64)
        for h in range(2):
            nc.scalar.copy(w_bf[:, :, h * P // 2 : (h + 1) * P // 2, :].rearrange("p t m j -> p m t j"), w_raw[h][:].rearrange("p j (m t) -> p m t j", t=PACK))
        half_gs = keep.tile([P, PACK], F32, name="half_gs")
        nc.scalar.activation(half_gs[:], gs_sb[:], ACT.Copy, scale=0.5)

        w_codes = keep.tile([P, H], U32, name="w_codes", align_bytes=64)
        w_scales = keep.tile([P, H], U8, name="w_scales", align_bytes=64)
        nc.vector.quantize_mx(out=w_codes[:].bitcast(FP8X4), scales=w_scales[:], in_=w_bf[:].rearrange("p t m j -> p (t m j)"))
        xq_words = gather_words(offs_sb, "xq_words", "xq_words")
        cb_words = gather_words_dealt(cb_sb, "cb_words", "w_bf")

        y_win, half_y, st_win = [], [], []
        for t in range(PACK):
            win = keep.tile([P, WIDE], F32, name=f"y_win{t}")
            rows = slice(t * P, (t + 1) * P)
            for n, cols in enumerate(halves if t == 0 else [slice(0, S)]):
                bank = psum.tile([P, S], F32, name=f"y_ps{t}_{n}", tag=f"bank{t + PACK * n}")
                nc.tensor.matmul_mx(out=bank[:, cols], lhsT=w_codes[:, rows].bitcast(FP8X4), lhsT_scale=w_scales[:, rows],
                                    rhs=xq_words[:, cols].bitcast(FP8X4), rhs_scale=xq_scales[:, cols], start=True, stop=True)
                nc.scalar.copy(win[:, cols], bank[:, cols])
            y_win.append(win)
        for t in range(PACK):
            tile = keep.tile([P, S], F32, name=f"half_y{t}", tag=f"half_y{t}", align_bytes=64)
            nc.scalar.activation(tile[:], y_win[t][:, :S], ACT.Copy, scale=half_gs[:, t : t + 1])
            half_y.append(tile)

        hop = []

        def fetch_y(t):
            tile = keep.tile([P, S], F32, name=f"hop{t}")
            nc.vector.tensor_copy(tile[:], y_win[t][:].indirect(n1_sb[:]))
            hop.append(tile)

        def larger(t):
            st = keep.tile([P, S], F32, name=f"st{t}", tag=f"st{t}")
            nc.vector.tensor_tensor(st[:], hop[t][:], y_win[t][:, :S], ALU.max)
            win = keep.tile([P, 768], F32, name=f"st_win{t}")
            nc.scalar.activation(win[:, :S], st[:], ACT.Copy, scale=gs_sb[:, t : t + 1])
            st_win.append(win)

        fetch_y(0)
        for t in range(1, PACK):
            fetch_y(t)
            larger(t - 1)
        larger(PACK - 1)

        z_bf = [keep.tile([P, HALF * PACK], BF16, name=f"z_bf{h}", tag=f"z_bf{h}", align_bytes=64) for h in range(2)]
        for n, piece in enumerate(PIECES):
            z32 = keep.tile([P, PACK, piece.stop - piece.start], F32, name=f"z32_{n}", tag=("z32", f"st{PACK - 1}")[n])
            for t in range(PACK):
                nc.vector.tensor_tensor(z32[:, t, :], st_win[t][:].indirect(n2_sb[:, piece.start // 16 : piece.stop // 16]), half_y[t][:, piece], ALU.subtract)
            for h, half in enumerate(halves):
                first, last = max(piece.start, half.start), min(piece.stop, half.stop)
                if first < last:
                    nc.scalar.copy(z_bf[h][:, PACK * (first - half.start) : PACK * (last - half.start)].rearrange("p (c i t) -> p c t i", i=4, t=PACK),
                                   z32[:, :, first - piece.start : last - piece.start].rearrange("p t (c i) -> p c t i", i=4))

        z_codes = keep.tile([P, S], U32, name="z_codes", align_bytes=64)
        z_scales = keep.tile([P, S], U8, name="z_scales", align_bytes=64)

        def quantise_z(h):
            nc.vector.quantize_mx(out=z_codes[:, halves[h]].bitcast(FP8X4), scales=z_scales[:, halves[h]], in_=z_bf[h][:])

        def score(words, scales, bank, t, cols):
            rows = slice(t * P, (t + 1) * P)
            nc.tensor.matmul_mx(out=bank[:, cols], lhsT=words[:, rows].bitcast(FP8X4), lhsT_scale=scales[:, rows],
                                rhs=z_codes[:, cols].bitcast(FP8X4), rhs_scale=z_scales[:, cols], start=True, stop=True)

        b_win = [keep.tile([P, WIDE], F32, name=f"b_win{t}") for t in range(PACK)]
        gate = [keep.tile([P, S], F32, name=f"gate{t}") for t in range(PACK)]

        def score_b(t, cols, bank_no):
            bank = psum.tile([P, S], F32, name=f"b_ps{t}_{cols.start}", tag=f"bank{bank_no}")
            score(cb_words, cb_scales, bank, t, cols)
            nc.scalar.activation(b_win[t][:, cols], bank[:, cols], ACT.Copy, scale=0.0625)
            nc.scalar.activation(gate[t][:, cols], bank[:, cols], ACT.Tanh, scale=0.0625)

        quantise_z(0)
        score_b(0, halves[0], 0)
        ca_scales_raw1 = gather_scales(ca_sb, "ca_scales_raw1", "half_y3", halves[1])
        quantise_z(1)
        score_b(0, halves[1], PACK)
        deal(ca_scales_raw1, ca_scales, halves[1])
        ca_words = gather_words_dealt(ca_sb, "ca_words", "z_bf1")

        out_rows = out.rearrange("(g t q) j -> t g q j", t=PACK, q=PACK)
        prod = []

        def b_side(t):
            if t > 0:
                score_b(t, slice(0, S), PACK + t)
            tile = keep.tile([P, S], F32, name=f"prod{t}")
            nc.vector.tensor_tensor(tile[:], b_win[t][:].indirect(n4_sb[:]), gate[t][:], ALU.mult)
            prod.append(tile)

        def a_side(t):
            bank = psum.tile([P, S], F32, name=f"a_ps{t}", tag=f"bank{(t + 1) % PACK}")
            score(ca_words, ca_scales, bank, t, slice(0, S))
            win = keep.tile([P, WIDE], F32, name=f"a_win{t}")
            nc.scalar.activation(win[:, :S], bank[:], ACT.Copy, scale=0.0625)
            for n, cols in enumerate(halves if t == PACK - 1 else [slice(0, S)]):
                res = keep.tile([P, cols.stop - cols.start], F32, name=f"res{t}_{n}")
                nc.vector.tensor_tensor(res[:], win[:].indirect(n3_sb[:, cols.start // 16 : cols.stop // 16]), prod[t][:, cols], ALU.subtract)
                nc.sync.dma_start(out_rows[t][:, :, cols], res[:])

        b_side(0)
        for t in range(1, PACK):
            b_side(t)
            a_side(t - 1)
        a_side(PACK - 1)
